import numpy as np
import ml_dtypes


def mxq(x, axis, fmt="e4m3"):
    dtype, down = {"e4m3": (ml_dtypes.float8_e4m3fn, 7), "e5m2": (ml_dtypes.float8_e5m2, 14)}[fmt]
    v = np.moveaxis(np.asarray(x, np.float32).astype(ml_dtypes.bfloat16).astype(np.float64), axis, -1)
    blocks = v.reshape(v.shape[:-1] + (-1, 32))
    amax = np.abs(blocks).max(-1, keepdims=True)
    byte = np.maximum(np.where(amax > 0, np.frexp(amax)[1] - 1 + 127, 0) - down, 1)
    scale = np.exp2(byte - 127.0)
    codes = (blocks / scale).astype(np.float32).astype(dtype).astype(np.float64)
    return np.moveaxis((codes * scale).reshape(v.shape), -1, axis)


WIDE = False


def mx_kscale(k):
    if not WIDE:
        return np.ones(k)
    levels = np.array([10, -10, 5, -5, 0])
    if k % 512:
        return np.exp2(np.random.permutation(np.resize(levels, k // 32))).repeat(32)
    a = np.empty((k // 512, 16))
    for p in range(k // 512):
        a[p, :8] = np.random.permutation(np.resize(levels, 8))
        for g in range(8):
            far = levels[np.abs(levels - a[p, g]) >= 10]
            a[p, g + 8] = far[np.random.randint(len(far))]
    return np.exp2(a.ravel()).repeat(32)


def f64(x):
    return np.asarray(x).astype(np.float64)


def striped(idx):
    return np.tile(idx.reshape(-1, 16).T, (8, 1)).astype(np.uint16)


def unstriped(offs):
    return offs[:16].T.reshape(-1).astype(np.int64)


E2M1 = np.array([0.0, 0.5, 1.0, 1.5, 2.0, 3.0, 4.0, 6.0, -0.0, -0.5, -1.0, -1.5, -2.0, -3.0, -4.0, -6.0])


def pack_weight(w, fmt):
    k, n = w.shape
    w = f64(np.asarray(w, np.float32).astype(ml_dtypes.bfloat16)).reshape(k // 32, 32, n)
    amax = np.abs(w).max(1)
    if fmt == "e4m3":
        byte = np.frexp(amax)[1] - 1 + 127 - 7
    else:
        mant, ex = np.frexp(amax / 6.0)
        byte = np.where(mant > 0.5, ex, ex - 1) + 127
    byte = np.clip(np.where(amax > 0, byte, 1), 1, 254)
    scaled = (w * np.exp2(127.0 - byte)[:, None, :]).reshape(k, n).astype(np.float32)
    by_word = np.ascontiguousarray(scaled.reshape(k // 512, 128, 4, n).transpose(0, 1, 3, 2))
    if fmt == "e4m3":
        words = by_word.astype(ml_dtypes.float8_e4m3fn).view(np.uint8)
    else:
        c = by_word.astype(ml_dtypes.float4_e2m1fn).view(np.uint8) & 0xF
        words = (c[..., 0::2] | (c[..., 1::2] << 4)).reshape(k // 512, 128, 2 * n)
    return np.ascontiguousarray(words), np.ascontiguousarray(byte.astype(np.uint8).reshape(k // 512, 16, n))


def unpack_weight(words, scales, fmt):
    g, _, n = scales.shape
    words = np.ascontiguousarray(words).reshape(g, 128, n, -1)
    if fmt == "e4m3":
        vals = words.view(ml_dtypes.float8_e4m3fn).astype(np.float64)
    else:
        nib = np.empty((g, 128, n, 4), np.uint8)
        nib[..., 0::2] = words & 0xF
        nib[..., 1::2] = words >> 4
        vals = E2M1[nib]
    vals = vals * np.repeat(np.exp2(scales.astype(np.float64) - 127.0), 8, axis=1)[..., None]
    return vals.transpose(0, 1, 3, 2).reshape(g * 512, n)


def gelu(v):
    return 0.5 * v * (1.0 + np.tanh(np.sqrt(2.0 / np.pi) * (v + 0.044715 * v**3)))


K, H, T, S, P = 1024, 512, 4096, 1024, 512


def setup_inputs():
    n = np.random.standard_normal
    s = mx_kscale(K)[:, None]
    u = mx_kscale(H)[:, None]
    tab_words, tab_scales = pack_weight(n((K, T)) * s, "e4m3")
    w4_words, w4_scales = pack_weight(n((H, H)) * 2.3 / np.sqrt(H) / u, "e2m1")
    return {
        "tab_words": tab_words, "tab_scales": tab_scales,
        "offs": striped(np.random.permutation(T)[:S]),
        "pos1": striped(np.random.permutation(S)[:P]),
        "w1": (n((K, H)) * 1.3 / np.sqrt(K) / s).astype(np.float32),
        "b1": (0.6 * n(H)).astype(np.float32),
        "gain": (np.exp(0.3 * n(H)) * u[:, 0]).astype(np.float32),
        "pigment": n((H, P)).astype(np.float32),
        "w4_words": w4_words, "w4_scales": w4_scales,
        "w2": (n((H, H)) * 2.3 / np.sqrt(H) / u).astype(np.float32),
        "skip": (np.exp(0.3 * n(H)) / u[:, 0]).astype(np.float32),
        "wgo": np.exp(0.3 * n((128, P))).astype(np.float32),
    }


def reference(tab_words, tab_scales, offs, pos1, w1, b1, gain, pigment, w4_words, w4_scales, w2, skip, wgo):
    v = unpack_weight(tab_words, tab_scales, "e4m3")[:, unstriped(offs)]
    w4 = unpack_weight(w4_words, w4_scales, "e2m1")
    pre = (mxq(f64(w1), 0, "e4m3").T @ v) + f64(b1)[:, None]
    h = np.tanh(pre) * f64(gain)[:, None]
    x = h[:, unstriped(pos1)]
    xq = mxq(x, 0, "e4m3")
    tinted = mxq(x * f64(pigment), 0, "e4m3")
    z = w4.T @ xq + mxq(f64(w2), 0, "e4m3").T @ tinted
    y = 1.0 / (1.0 + np.exp(-z))
    out = f64(skip)[:, None] * h
    out[:, unstriped(pos1)] = np.tile(f64(wgo), (H // 128, 1)) * y
    return out

@@ -1,0 +1,238 @@
+from contextlib import ExitStack
+
+import concourse.mybir as mybir
+
+K, H, T, S, M = 1024, 512, 4096, 1024, 512
+FLOPS = 2 * K * H * S + 2 * 2 * H * H * M
+
+F32 = mybir.dt.float32
+BF16 = mybir.dt.bfloat16
+I32 = mybir.dt.int32
+U32 = mybir.dt.uint32
+U16 = mybir.dt.uint16
+U8 = mybir.dt.uint8
+FP8X4 = mybir.dt.float8_e4m3fn_x4
+FP4X4 = mybir.dt.float4_e2m1fn_x4
+MULT = mybir.AluOpType.mult
+ACT = mybir.ActivationFunctionType
+
+P = 128
+PACK = 4
+HALVES = 2
+S_HALF = S // HALVES
+M_HALF = M // HALVES
+LIST_ROWS = 16
+
+
+def deal_weight(engine_copy, raw, grouped, col0, cols):
+    engine_copy(
+        grouped[:, :, col0 : col0 + cols].rearrange("p t (mm mi j) -> p mm j mi t", mi=2, j=PACK),
+        raw[:].rearrange("p j (mm mi t) -> p mm j mi t", mi=2, t=PACK),
+    )
+
+
+def tile_list_fresco_loss_inpainting_kernel(
+    tc, tab_words, tab_scales, offs, pos1, w1, b1, gain, pigment, w4_words, w4_scales, w2, skip, wgo, out
+):
+    nc = tc.nc
+    with ExitStack() as ctx:
+        lists = ctx.enter_context(tc.tile_pool(name="lists", bufs=1))
+        sb = ctx.enter_context(tc.tile_pool(name="sb", bufs=1))
+        psum = ctx.enter_context(tc.psum_pool(name="psum", bufs=1))
+
+        def tile(shape, dtype, name, tag=None):
+            return sb.tile(shape, dtype, name=name, tag=tag or name, align_bytes=64)
+
+        offs_sb = lists.tile([P, S // LIST_ROWS], U16, name="offs_sb")
+        pos_sb = lists.tile([P, M // LIST_ROWS], U16, name="pos_sb")
+
+        tab_plane = tile([P, T], U8, "tab_plane")
+        w4_plane_raw = tile([P, H], U8, "w4_plane_raw")
+        nc.vector.memset(tab_plane[:].bitcast(I32), 0)
+        nc.vector.memset(w4_plane_raw[:].bitcast(I32), 0)
+
+        tab_sb = [tile([P, T], U32, "tab_sb%d" % a) for a in range(2)]
+        w1_raw0 = tile([P, PACK, H], F32, "w1_raw0")
+        w1_raw1 = [tile([P, PACK, H // 2], F32, "w1_raw1_%d" % c) for c in range(2)]
+        w1_rows = w1.rearrange("(a p j) r -> a p j r", p=P, j=PACK)
+        b1_sb = tile([P, PACK], F32, "b1_sb")
+        gain_sb = tile([P, PACK], F32, "gain_sb")
+        skip_sb = tile([P, PACK], F32, "skip_sb")
+        w4_raw = tile([P, 2 * H], U8, "w4_raw")
+        pig_sb = tile([P, PACK, M], F32, "pig_sb")
+        w2_raw = tile([P, PACK, H], F32, "w2_raw")
+        wgo_sb = tile([P, PACK * M], F32, "wgo_sb")
+
+        def tab_pass(a):
+            return tab_words[a].rearrange("p n i -> p (n i)").bitcast(I32)
+
+        nc.sync.dma_start(offs_sb[:], offs)
+        nc.sync.dma_start(tab_sb[0][:].bitcast(I32), tab_pass(0))
+        nc.sync.dma_start(w1_raw0[:], w1_rows[0])
+        nc.sync.dma_start(tab_sb[1][:].bitcast(I32), tab_pass(1))
+        for q in range(4):
+            nc.gpsimd.dma_start(
+                tab_plane[32 * q : 32 * q + 8, :].bitcast(I32), tab_scales[:, 4 * q : 4 * q + 4, :].bitcast(I32)
+            )
+        nc.scalar.dma_start(w4_raw[:].bitcast(I32), w4_words[0].bitcast(I32))
+        for vec_sb, vec in ((b1_sb, b1), (gain_sb, gain), (skip_sb, skip)):
+            nc.scalar.dma_start(vec_sb[:], vec.rearrange("(p t) -> p t", t=PACK))
+        for c in range(2):
+            nc.sync.dma_start(w1_raw1[c][:], w1_rows[1][:, :, c * (H // 2) : (c + 1) * (H // 2)])
+        nc.sync.dma_start(pos_sb[:], pos1)
+        for q in range(4):
+            nc.sync.dma_start(
+                w4_plane_raw[32 * q : 32 * q + 4, :].bitcast(I32), w4_scales[0, 4 * q : 4 * q + 4, :].bitcast(I32)
+            )
+        nc.sync.dma_start(pig_sb[:], pigment.rearrange("(p t) m -> p t m", t=PACK))
+        nc.sync.dma_start(w2_raw[:], w2.rearrange("(p j) n -> p j n", j=PACK))
+        wgo_rows = wgo.rearrange("(q t) m -> q (t m)", t=PACK)
+        for q in range(4):
+            nc.sync.dma_start(wgo_sb[32 * q : 32 * (q + 1), :], wgo_rows)
+
+        w4_codes = tile([P, 2 * H], U8, "w4_codes")
+        nc.vector.tensor_copy(
+            w4_codes[:].rearrange("p (t m b) -> p t m b", t=PACK, b=2),
+            w4_raw[:].rearrange("p (m t b) -> p t m b", t=PACK, b=2),
+        )
+
+        def offs_half(c):
+            n = S_HALF // LIST_ROWS
+            return offs_sb[:, c * n : (c + 1) * n]
+
+        def pos_half(c):
+            n = M_HALF // LIST_ROWS
+            return pos_sb[:, c * n : (c + 1) * n]
+
+        v_codes = {}
+        for c in range(HALVES):
+            v_half = tile([P, S_HALF], U32, "v_codes0_%d" % c)
+            v_codes[0, c] = v_half[:]
+            nc.vector.tensor_copy(v_codes[0, c], tab_sb[0][:].indirect(offs_half(c)))
+        v_plane = tile([P, S], U8, "v_plane")
+        nc.vector.tensor_copy(v_plane[:], tab_plane[:].indirect(offs_sb[:]))
+
+        w1_bf = [tile([P, PACK, H], BF16, "w1_bf%d" % a) for a in range(2)]
+        w1_codes = [tile([P, H], U32, "w1_codes%d" % a) for a in range(2)]
+        w1_plane = [tile([P, H], U8, "w1_plane%d" % a) for a in range(2)]
+        deal_weight(nc.scalar.copy, w1_raw0, w1_bf[0], 0, H)
+        nc.vector.quantize_mx(
+            w1_codes[0][:].bitcast(FP8X4), w1_plane[0][:], w1_bf[0][:].rearrange("p t x -> p (t x)")
+        )
+
+        pre = {}
+
+        def first_product(a, t, c):
+            cols = slice(t * P, (t + 1) * P)
+            nc.tensor.matmul_mx(
+                pre[t, c][:],
+                lhsT=w1_codes[a][:, cols].bitcast(FP8X4),
+                lhsT_scale=w1_plane[a][:, cols],
+                rhs=v_codes[a, c].bitcast(FP8X4),
+                rhs_scale=v_plane[4 * a : P, c * S_HALF : (c + 1) * S_HALF],
+                start=(a == 0),
+                stop=(a == 1),
+            )
+
+        for t in range(PACK):
+            for c in range(HALVES):
+                pre[t, c] = psum.tile([P, S_HALF], F32, name="pre%d_%d" % (t, c), tag="bank%d_%d" % (t, c))
+                first_product(0, t, c)
+
+        v_codes1 = tile([P, S], U32, "v_codes1", tag="tab_plane")
+        for c in range(HALVES):
+            v_codes[1, c] = v_codes1[:, c * S_HALF : (c + 1) * S_HALF]
+            nc.vector.tensor_copy(v_codes[1, c], tab_sb[1][:].indirect(offs_half(c)))
+        deal_weight(nc.scalar.copy, w1_raw1[0], w1_bf[1], 0, H // 2)
+        deal_weight(nc.vector.tensor_copy, w1_raw1[1], w1_bf[1], H // 2, H // 2)
+        for t in range(PACK):
+            cols = slice(t * P, (t + 1) * P)
+            nc.vector.quantize_mx(w1_codes[1][:, cols].bitcast(FP8X4), w1_plane[1][:, cols], w1_bf[1][:, t, :])
+            for c in range(HALVES):
+                first_product(1, t, c)
+
+        w4_plane = tile([P, H], U8, "w4_plane")
+        nc.vector.tensor_copy(
+            w4_plane[:].rearrange("p (t m) -> p t m", t=PACK),
+            w4_plane_raw[:].rearrange("p (m t) -> p t m", t=PACK),
+        )
+
+        h = [tile([P, S], F32, "h%d" % t) for t in range(PACK)]
+        x32 = [tile([P, PACK, M_HALF], F32, "x32_%d" % c) for c in range(HALVES)]
+        for t in range(PACK):
+            for c in range(HALVES):
+                cols = slice(c * S_HALF, (c + 1) * S_HALF)
+                nc.scalar.activation(h[t][:, cols], pre[t, c][:], ACT.Tanh, bias=b1_sb[:, t : t + 1])
+                if t < PACK - 1:
+                    nc.vector.tensor_scalar(h[t][:, cols], h[t][:, cols], gain_sb[:, t : t + 1], None, MULT)
+            if t == PACK - 1:
+                nc.scalar.activation(h[t][:], h[t][:], ACT.Copy, scale=gain_sb[:, t : t + 1])
+            for c in range(HALVES):
+                nc.vector.tensor_copy(x32[c][:, t, :], h[t][:].indirect(pos_half(c)))
+
+        w2_bf = tile([P, PACK, H], BF16, "w2_bf")
+        w2_codes = tile([P, H], U32, "w2_codes")
+        w2_plane = tile([P, H], U8, "w2_plane")
+        deal_weight(nc.scalar.copy, w2_raw, w2_bf, 0, H)
+        nc.vector.quantize_mx(w2_codes[:].bitcast(FP8X4), w2_plane[:], w2_bf[:].rearrange("p t x -> p (t x)"))
+
+        page = [tile([P, S], F32, "page%d" % t) for t in range(PACK)]
+
+        def fill_page(t):
+            nc.scalar.activation(page[t][:], h[t][:], ACT.Copy, scale=skip_sb[:, t : t + 1])
+
+        fill_page(0)
+
+        z = {}
+        for c in range(HALVES):
+            cols = slice(c * M_HALF, (c + 1) * M_HALF)
+            x_bf = tile([P, PACK * M_HALF], BF16, "x_bf%d" % c)
+            tint_bf = tile([P, PACK * M_HALF], BF16, "tint_bf%d" % c)
+            x_planes = x32[c][:].rearrange("p t (g i) -> p g t i", i=4)
+            nc.scalar.copy(x_bf[:].rearrange("p (g i t) -> p g t i", i=4, t=PACK), x_planes)
+            nc.vector.tensor_tensor(
+                tint_bf[:].rearrange("p (g i t) -> p g t i", i=4, t=PACK),
+                x_planes,
+                pig_sb[:, :, cols].rearrange("p t (g i) -> p g t i", i=4),
+                MULT,
+            )
+            x_codes = tile([P, M_HALF], U32, "x_codes%d" % c)
+            x_plane = tile([P, M_HALF], U8, "x_plane%d" % c)
+            tint_codes = tile([P, M_HALF], U32, "tint_codes%d" % c)
+            tint_plane = tile([P, M_HALF], U8, "tint_plane%d" % c)
+            nc.vector.quantize_mx(x_codes[:].bitcast(FP8X4), x_plane[:], x_bf[:])
+            nc.vector.quantize_mx(tint_codes[:].bitcast(FP8X4), tint_plane[:], tint_bf[:])
+            for t in range(PACK):
+                z[t, c] = psum.tile([P, M_HALF], F32, name="z%d_%d" % (t, c), tag="bank%d_%d" % (t, c))
+                nc.tensor.matmul_mx(
+                    z[t, c][:],
+                    lhsT=w4_codes[:, 2 * P * t : 2 * P * (t + 1)].bitcast(FP4X4),
+                    lhsT_scale=w4_plane[:, P * t : P * (t + 1)],
+                    rhs=x_codes[:].bitcast(FP8X4),
+                    rhs_scale=x_plane[:],
+                    start=True,
+                    stop=False,
+                )
+                nc.tensor.matmul_mx(
+                    z[t, c][:],
+                    lhsT=w2_codes[:, P * t : P * (t + 1)].bitcast(FP8X4),
+                    lhsT_scale=w2_plane[:, P * t : P * (t + 1)],
+                    rhs=tint_codes[:].bitcast(FP8X4),
+                    rhs_scale=tint_plane[:],
+                    start=False,
+                    stop=True,
+                )
+
+        out_rows = out.rearrange("(p t) j -> p t j", t=PACK)
+        for t in range(PACK):
+            if t > 0:
+                fill_page(t)
+            for c in range(HALVES):
+                y = tile([P, M_HALF], F32, "y%d_%d" % (t, c))
+                nc.scalar.activation(y[:], z[t, c][:], ACT.Tanh, scale=0.5)
+                nc.scalar.activation(y[:], y[:], ACT.Copy, bias=0.5, scale=0.5)
+                col0 = t * M + c * M_HALF
+                nc.vector.tensor_tensor(
+                    page[t][:].indirect(pos_half(c)), y[:], wgo_sb[:, col0 : col0 + M_HALF], MULT
+                )
+            nc.sync.dma_start(out_rows[:, t, :], page[t][:])

@@ -49,7 +49,7 @@ def tile_list_fresco_loss_inpainting_kernel(
         tab_plane = tile([P, T], U8, "tab_plane")
         w4_plane_raw = tile([P, H], U8, "w4_plane_raw")
         nc.vector.memset(tab_plane[:].bitcast(I32), 0)
-        nc.vector.memset(w4_plane_raw[:].bitcast(I32), 0)
+        nc.gpsimd.memset(w4_plane_raw[:].bitcast(I32), 0)
 
         tab_sb = [tile([P, T], U32, "tab_sb%d" % a) for a in range(2)]
         w1_raw0 = tile([P, PACK, H], F32, "w1_raw0")
@@ -60,49 +60,55 @@ def tile_list_fresco_loss_inpainting_kernel(
         skip_sb = tile([P, PACK], F32, "skip_sb")
         w4_raw = tile([P, 2 * H], U8, "w4_raw")
         pig_sb = tile([P, PACK, M], F32, "pig_sb")
-        w2_raw = tile([P, PACK, H], F32, "w2_raw")
+        w2_raw = [tile([P, PACK, H // 2], F32, "w2_raw%d" % c) for c in range(2)]
+        w2_rows = w2.rearrange("(p j) n -> p j n", j=PACK)
         wgo_sb = tile([P, PACK * M], F32, "wgo_sb")
 
         def tab_pass(a):
             return tab_words[a].rearrange("p n i -> p (n i)").bitcast(I32)
 
+        tab_rows = tile([P, T], U8, "tab_rows")
+
+        def load_tab_scales(a):
+            for r in range(4):
+                nc.sync.dma_start(tab_rows[4 * a + r : P : 32, :].bitcast(I32), tab_scales[a, r:16:4, :].bitcast(I32))
+
+        for a in range(2):
+            load_tab_scales(a)
+            if a == 0:
+                nc.sync.dma_start(tab_sb[0][:, : T // 2].bitcast(I32), tab_pass(0)[:, : T // 2])
+        nc.sync.dma_start(tab_sb[0][:, T // 2 :].bitcast(I32), tab_pass(0)[:, T // 2 :])
         nc.sync.dma_start(offs_sb[:], offs)
-        nc.sync.dma_start(tab_sb[0][:].bitcast(I32), tab_pass(0))
         nc.sync.dma_start(w1_raw0[:], w1_rows[0])
         nc.sync.dma_start(tab_sb[1][:].bitcast(I32), tab_pass(1))
-        for q in range(4):
-            nc.gpsimd.dma_start(
-                tab_plane[32 * q : 32 * q + 8, :].bitcast(I32), tab_scales[:, 4 * q : 4 * q + 4, :].bitcast(I32)
-            )
-        nc.scalar.dma_start(w4_raw[:].bitcast(I32), w4_words[0].bitcast(I32))
         for vec_sb, vec in ((b1_sb, b1), (gain_sb, gain), (skip_sb, skip)):
-            nc.scalar.dma_start(vec_sb[:], vec.rearrange("(p t) -> p t", t=PACK))
+            nc.gpsimd.dma_start(vec_sb[:], vec.rearrange("(p t) -> p t", t=PACK))
+        nc.gpsimd.dma_start(w4_raw[:].bitcast(I32), w4_words[0].bitcast(I32))
+        for r in range(4):
+            nc.gpsimd.dma_start(w4_plane_raw[r:P:32, :].bitcast(I32), w4_scales[0, r:16:4, :].bitcast(I32))
         for c in range(2):
             nc.sync.dma_start(w1_raw1[c][:], w1_rows[1][:, :, c * (H // 2) : (c + 1) * (H // 2)])
         nc.sync.dma_start(pos_sb[:], pos1)
-        for q in range(4):
-            nc.sync.dma_start(
-                w4_plane_raw[32 * q : 32 * q + 4, :].bitcast(I32), w4_scales[0, 4 * q : 4 * q + 4, :].bitcast(I32)
-            )
+        for c in range(2):
+            nc.sync.dma_start(w2_raw[c][:], w2_rows[:, :, c * (H // 2) : (c + 1) * (H // 2)])
         nc.sync.dma_start(pig_sb[:], pigment.rearrange("(p t) m -> p t m", t=PACK))
-        nc.sync.dma_start(w2_raw[:], w2.rearrange("(p j) n -> p j n", j=PACK))
         wgo_rows = wgo.rearrange("(q t) m -> q (t m)", t=PACK)
         for q in range(4):
             nc.sync.dma_start(wgo_sb[32 * q : 32 * (q + 1), :], wgo_rows)
 
         w4_codes = tile([P, 2 * H], U8, "w4_codes")
-        nc.vector.tensor_copy(
+        nc.gpsimd.tensor_copy(
             w4_codes[:].rearrange("p (t m b) -> p t m b", t=PACK, b=2),
             w4_raw[:].rearrange("p (m t b) -> p t m b", t=PACK, b=2),
         )
 
+        for q in range(4):
+            live = slice(32 * q, 32 * q + 8)
+            nc.vector.tensor_copy(tab_plane[live, :].bitcast(I32), tab_rows[live, :].bitcast(I32))
+
         def offs_half(c):
             n = S_HALF // LIST_ROWS
             return offs_sb[:, c * n : (c + 1) * n]
-
-        def pos_half(c):
-            n = M_HALF // LIST_ROWS
-            return pos_sb[:, c * n : (c + 1) * n]
 
         v_codes = {}
         for c in range(HALVES):
@@ -145,71 +151,75 @@ def tile_list_fresco_loss_inpainting_kernel(
             nc.vector.tensor_copy(v_codes[1, c], tab_sb[1][:].indirect(offs_half(c)))
         deal_weight(nc.scalar.copy, w1_raw1[0], w1_bf[1], 0, H // 2)
         deal_weight(nc.vector.tensor_copy, w1_raw1[1], w1_bf[1], H // 2, H // 2)
-        for t in range(PACK):
-            cols = slice(t * P, (t + 1) * P)
-            nc.vector.quantize_mx(w1_codes[1][:, cols].bitcast(FP8X4), w1_plane[1][:, cols], w1_bf[1][:, t, :])
-            for c in range(HALVES):
-                first_product(1, t, c)
+        for t0, t1 in ((0, 1), (1, PACK)):
+            cols = slice(t0 * P, t1 * P)
+            nc.vector.quantize_mx(
+                w1_codes[1][:, cols].bitcast(FP8X4),
+                w1_plane[1][:, cols],
+                w1_bf[1][:, t0:t1, :].rearrange("p t x -> p (t x)"),
+            )
+            for t in range(t0, t1):
+                for c in range(HALVES):
+                    first_product(1, t, c)
 
         w4_plane = tile([P, H], U8, "w4_plane")
-        nc.vector.tensor_copy(
+        nc.gpsimd.tensor_copy(
             w4_plane[:].rearrange("p (t m) -> p t m", t=PACK),
             w4_plane_raw[:].rearrange("p (m t) -> p t m", t=PACK),
         )
 
+        w2_bf = tile([P, PACK, H], BF16, "w2_bf")
+        deal_weight(nc.vector.tensor_copy, w2_raw[0], w2_bf, 0, H // 2)
+
         h = [tile([P, S], F32, "h%d" % t) for t in range(PACK)]
-        x32 = [tile([P, PACK, M_HALF], F32, "x32_%d" % c) for c in range(HALVES)]
+        x32 = tile([P, PACK, M], F32, "x32")
         for t in range(PACK):
+            gain_t = gain_sb[:, t : t + 1]
             for c in range(HALVES):
                 cols = slice(c * S_HALF, (c + 1) * S_HALF)
                 nc.scalar.activation(h[t][:, cols], pre[t, c][:], ACT.Tanh, bias=b1_sb[:, t : t + 1])
-                if t < PACK - 1:
-                    nc.vector.tensor_scalar(h[t][:, cols], h[t][:, cols], gain_sb[:, t : t + 1], None, MULT)
+                if t == 0:
+                    nc.vector.tensor_scalar(h[t][:, cols], h[t][:, cols], gain_t, None, MULT)
             if t == PACK - 1:
-                nc.scalar.activation(h[t][:], h[t][:], ACT.Copy, scale=gain_sb[:, t : t + 1])
-            for c in range(HALVES):
-                nc.vector.tensor_copy(x32[c][:, t, :], h[t][:].indirect(pos_half(c)))
+                for c in range(HALVES):
+                    cols = slice(c * S_HALF, (c + 1) * S_HALF)
+                    nc.scalar.activation(h[t][:, cols], h[t][:, cols], ACT.Copy, scale=gain_t)
+            elif t > 0:
+                nc.vector.tensor_scalar(h[t][:], h[t][:], gain_t, None, MULT)
+            nc.vector.tensor_copy(x32[:, t, :], h[t][:].indirect(pos_sb[:]))
 
-        w2_bf = tile([P, PACK, H], BF16, "w2_bf")
         w2_codes = tile([P, H], U32, "w2_codes")
         w2_plane = tile([P, H], U8, "w2_plane")
-        deal_weight(nc.scalar.copy, w2_raw, w2_bf, 0, H)
+        deal_weight(nc.scalar.copy, w2_raw[1], w2_bf, H // 2, H // 2)
         nc.vector.quantize_mx(w2_codes[:].bitcast(FP8X4), w2_plane[:], w2_bf[:].rearrange("p t x -> p (t x)"))
-
-        page = [tile([P, S], F32, "page%d" % t) for t in range(PACK)]
-
-        def fill_page(t):
-            nc.scalar.activation(page[t][:], h[t][:], ACT.Copy, scale=skip_sb[:, t : t + 1])
-
-        fill_page(0)
 
         z = {}
         for c in range(HALVES):
             cols = slice(c * M_HALF, (c + 1) * M_HALF)
-            x_bf = tile([P, PACK * M_HALF], BF16, "x_bf%d" % c)
-            tint_bf = tile([P, PACK * M_HALF], BF16, "tint_bf%d" % c)
-            x_planes = x32[c][:].rearrange("p t (g i) -> p g t i", i=4)
-            nc.scalar.copy(x_bf[:].rearrange("p (g i t) -> p g t i", i=4, t=PACK), x_planes)
+            both_bf = tile([P, 2, PACK * M_HALF], BF16, "both_bf%d" % c)
+            x_planes = x32[:, :, cols].rearrange("p t (g i) -> p g t i", i=4)
+            nc.scalar.copy(both_bf[:, 0, :].rearrange("p (g i t) -> p g t i", i=4, t=PACK), x_planes)
             nc.vector.tensor_tensor(
-                tint_bf[:].rearrange("p (g i t) -> p g t i", i=4, t=PACK),
+                both_bf[:, 1, :].rearrange("p (g i t) -> p g t i", i=4, t=PACK),
                 x_planes,
                 pig_sb[:, :, cols].rearrange("p t (g i) -> p g t i", i=4),
                 MULT,
             )
-            x_codes = tile([P, M_HALF], U32, "x_codes%d" % c)
-            x_plane = tile([P, M_HALF], U8, "x_plane%d" % c)
-            tint_codes = tile([P, M_HALF], U32, "tint_codes%d" % c)
-            tint_plane = tile([P, M_HALF], U8, "tint_plane%d" % c)
-            nc.vector.quantize_mx(x_codes[:].bitcast(FP8X4), x_plane[:], x_bf[:])
-            nc.vector.quantize_mx(tint_codes[:].bitcast(FP8X4), tint_plane[:], tint_bf[:])
+            both_codes = tile([P, 2, M_HALF], U32, "both_codes%d" % c)
+            both_plane = tile([P, 2, M_HALF], U8, "both_plane%d" % c)
+            nc.vector.quantize_mx(
+                both_codes[:].rearrange("p s m -> p (s m)").bitcast(FP8X4),
+                both_plane[:].rearrange("p s m -> p (s m)"),
+                both_bf[:].rearrange("p s x -> p (s x)"),
+            )
             for t in range(PACK):
                 z[t, c] = psum.tile([P, M_HALF], F32, name="z%d_%d" % (t, c), tag="bank%d_%d" % (t, c))
                 nc.tensor.matmul_mx(
                     z[t, c][:],
                     lhsT=w4_codes[:, 2 * P * t : 2 * P * (t + 1)].bitcast(FP4X4),
                     lhsT_scale=w4_plane[:, P * t : P * (t + 1)],
-                    rhs=x_codes[:].bitcast(FP8X4),
-                    rhs_scale=x_plane[:],
+                    rhs=both_codes[:, 0, :].bitcast(FP8X4),
+                    rhs_scale=both_plane[:, 0, :],
                     start=True,
                     stop=False,
                 )
@@ -217,22 +227,28 @@ def tile_list_fresco_loss_inpainting_kernel(
                     z[t, c][:],
                     lhsT=w2_codes[:, P * t : P * (t + 1)].bitcast(FP8X4),
                     lhsT_scale=w2_plane[:, P * t : P * (t + 1)],
-                    rhs=tint_codes[:].bitcast(FP8X4),
-                    rhs_scale=tint_plane[:],
+                    rhs=both_codes[:, 1, :].bitcast(FP8X4),
+                    rhs_scale=both_plane[:, 1, :],
                     start=False,
                     stop=True,
                 )
 
         out_rows = out.rearrange("(p t) j -> p t j", t=PACK)
         for t in range(PACK):
-            if t > 0:
-                fill_page(t)
-            for c in range(HALVES):
-                y = tile([P, M_HALF], F32, "y%d_%d" % (t, c))
-                nc.scalar.activation(y[:], z[t, c][:], ACT.Tanh, scale=0.5)
-                nc.scalar.activation(y[:], y[:], ACT.Copy, bias=0.5, scale=0.5)
-                col0 = t * M + c * M_HALF
+            page = tile([P, S], F32, "page%d" % t, tag="w2_bf" if t == 0 else "half_tanh%d" % (t - 1))
+            nc.scalar.activation(page[:], h[t][:], ACT.Copy, scale=skip_sb[:, t : t + 1])
+            half_tanh = tile([P, M], F32, "half_tanh%d" % t)
+            y = tile([P, M], F32, "y%d" % t)
+            pieces = [(c, c + 1) for c in range(HALVES)] if t == 0 else [(0, HALVES)]
+            for c0, c1 in pieces:
+                for c in range(c0, c1):
+                    nc.scalar.activation(half_tanh[:, c * M_HALF : (c + 1) * M_HALF], z[t, c][:], ACT.Tanh, scale=0.5)
+                cols = slice(c0 * M_HALF, c1 * M_HALF)
+                nc.scalar.activation(y[:, cols], half_tanh[:, cols], ACT.Copy, bias=0.5, scale=0.5)
                 nc.vector.tensor_tensor(
-                    page[t][:].indirect(pos_half(c)), y[:], wgo_sb[:, col0 : col0 + M_HALF], MULT
+                    page[:].indirect(pos_sb[:, c0 * M_HALF // LIST_ROWS : c1 * M_HALF // LIST_ROWS]),
+                    y[:, cols],
+                    wgo_sb[:, t * M + c0 * M_HALF : t * M + c1 * M_HALF],
+                    MULT,
                 )
-            nc.sync.dma_start(out_rows[:, t, :], page[t][:])
+            nc.sync.dma_start(out_rows[:, t, :], page[:])

@@ -24,10 +24,10 @@ M_HALF = M // HALVES
 LIST_ROWS = 16
 
 
-def deal_weight(engine_copy, raw, grouped, col0, cols):
+def deal_weight(engine_copy, raw, grouped, col0, cols, order):
     engine_copy(
-        grouped[:, :, col0 : col0 + cols].rearrange("p t (mm mi j) -> p mm j mi t", mi=2, j=PACK),
-        raw[:].rearrange("p j (mm mi t) -> p mm j mi t", mi=2, t=PACK),
+        grouped[:, :, col0 : col0 + cols].rearrange("p (u e) (m j) -> " + order, e=2, j=PACK),
+        raw[:].rearrange("p j (m u e) -> " + order, u=2, e=2),
     )
 
 
@@ -52,8 +52,7 @@ def tile_list_fresco_loss_inpainting_kernel(
         nc.gpsimd.memset(w4_plane_raw[:].bitcast(I32), 0)
 
         tab_sb = [tile([P, T], U32, "tab_sb%d" % a) for a in range(2)]
-        w1_raw0 = tile([P, PACK, H], F32, "w1_raw0")
-        w1_raw1 = [tile([P, PACK, H // 2], F32, "w1_raw1_%d" % c) for c in range(2)]
+        w1_raw = [tile([P, PACK, H], F32, "w1_raw%d" % a) for a in range(2)]
         w1_rows = w1.rearrange("(a p j) r -> a p j r", p=P, j=PACK)
         b1_sb = tile([P, PACK], F32, "b1_sb")
         gain_sb = tile([P, PACK], F32, "gain_sb")
@@ -67,159 +66,144 @@ def tile_list_fresco_loss_inpainting_kernel(
         def tab_pass(a):
             return tab_words[a].rearrange("p n i -> p (n i)").bitcast(I32)
 
-        tab_rows = tile([P, T], U8, "tab_rows")
-
-        def load_tab_scales(a):
-            for r in range(4):
-                nc.sync.dma_start(tab_rows[4 * a + r : P : 32, :].bitcast(I32), tab_scales[a, r:16:4, :].bitcast(I32))
-
         for a in range(2):
-            load_tab_scales(a)
-            if a == 0:
-                nc.sync.dma_start(tab_sb[0][:, : T // 2].bitcast(I32), tab_pass(0)[:, : T // 2])
-        nc.sync.dma_start(tab_sb[0][:, T // 2 :].bitcast(I32), tab_pass(0)[:, T // 2 :])
+            nc.sync.dma_start(w1_raw[a][:], w1_rows[a])
         nc.sync.dma_start(offs_sb[:], offs)
-        nc.sync.dma_start(w1_raw0[:], w1_rows[0])
-        nc.sync.dma_start(tab_sb[1][:].bitcast(I32), tab_pass(1))
-        for vec_sb, vec in ((b1_sb, b1), (gain_sb, gain), (skip_sb, skip)):
-            nc.gpsimd.dma_start(vec_sb[:], vec.rearrange("(p t) -> p t", t=PACK))
+        for a in range(2):
+            nc.sync.dma_start(tab_sb[a][:].bitcast(I32), tab_pass(a))
+        for q in range(4):
+            nc.gpsimd.dma_start(
+                tab_plane[32 * q : 32 * q + 8, :].bitcast(I32), tab_scales[:, 4 * q : 4 * q + 4, :].bitcast(I32)
+            )
         nc.gpsimd.dma_start(w4_raw[:].bitcast(I32), w4_words[0].bitcast(I32))
         for r in range(4):
             nc.gpsimd.dma_start(w4_plane_raw[r:P:32, :].bitcast(I32), w4_scales[0, r:16:4, :].bitcast(I32))
-        for c in range(2):
-            nc.sync.dma_start(w1_raw1[c][:], w1_rows[1][:, :, c * (H // 2) : (c + 1) * (H // 2)])
+        for vec_sb, vec in ((b1_sb, b1), (gain_sb, gain), (skip_sb, skip)):
+            nc.sync.dma_start(vec_sb[:], vec.rearrange("(p t) -> p t", t=PACK))
         nc.sync.dma_start(pos_sb[:], pos1)
-        for c in range(2):
-            nc.sync.dma_start(w2_raw[c][:], w2_rows[:, :, c * (H // 2) : (c + 1) * (H // 2)])
+        nc.sync.dma_start(w2_raw[0][:], w2_rows[:, :, : H // 2])
         nc.sync.dma_start(pig_sb[:], pigment.rearrange("(p t) m -> p t m", t=PACK))
+        nc.sync.dma_start(w2_raw[1][:], w2_rows[:, :, H // 2 :])
         wgo_rows = wgo.rearrange("(q t) m -> q (t m)", t=PACK)
         for q in range(4):
             nc.sync.dma_start(wgo_sb[32 * q : 32 * (q + 1), :], wgo_rows)
-
-        w4_codes = tile([P, 2 * H], U8, "w4_codes")
-        nc.gpsimd.tensor_copy(
-            w4_codes[:].rearrange("p (t m b) -> p t m b", t=PACK, b=2),
-            w4_raw[:].rearrange("p (m t b) -> p t m b", t=PACK, b=2),
-        )
-
-        for q in range(4):
-            live = slice(32 * q, 32 * q + 8)
-            nc.vector.tensor_copy(tab_plane[live, :].bitcast(I32), tab_rows[live, :].bitcast(I32))
 
         def offs_half(c):
             n = S_HALF // LIST_ROWS
             return offs_sb[:, c * n : (c + 1) * n]
 
-        v_codes = {}
-        for c in range(HALVES):
-            v_half = tile([P, S_HALF], U32, "v_codes0_%d" % c)
-            v_codes[0, c] = v_half[:]
-            nc.vector.tensor_copy(v_codes[0, c], tab_sb[0][:].indirect(offs_half(c)))
         v_plane = tile([P, S], U8, "v_plane")
         nc.vector.tensor_copy(v_plane[:], tab_plane[:].indirect(offs_sb[:]))
 
-        w1_bf = [tile([P, PACK, H], BF16, "w1_bf%d" % a) for a in range(2)]
         w1_codes = [tile([P, H], U32, "w1_codes%d" % a) for a in range(2)]
         w1_plane = [tile([P, H], U8, "w1_plane%d" % a) for a in range(2)]
-        deal_weight(nc.scalar.copy, w1_raw0, w1_bf[0], 0, H)
-        nc.vector.quantize_mx(
-            w1_codes[0][:].bitcast(FP8X4), w1_plane[0][:], w1_bf[0][:].rearrange("p t x -> p (t x)")
+        for a in range(2):
+            w1_bf = tile([P, PACK, H], BF16, "w1_bf%d" % a)
+            deal_weight(nc.scalar.copy, w1_raw[a], w1_bf, 0, H, "p u m j e")
+            nc.vector.quantize_mx(w1_codes[a][:].bitcast(FP8X4), w1_plane[a][:], w1_bf[:].rearrange("p t x -> p (t x)"))
+
+        w4_dealt = tile([P, 3 * H], U8, "w4_dealt", tag="tab_sb0")
+        w4_codes = w4_dealt[:, : 2 * H]
+        w4_plane = w4_dealt[:, 2 * H :]
+        nc.vector.tensor_copy(
+            w4_codes.bitcast(U16).rearrange("p (t m) -> p t m", t=PACK),
+            w4_raw[:].bitcast(U16).rearrange("p (m t) -> p t m", t=PACK),
         )
-
-        pre = {}
-
-        def first_product(a, t, c):
-            cols = slice(t * P, (t + 1) * P)
-            nc.tensor.matmul_mx(
-                pre[t, c][:],
-                lhsT=w1_codes[a][:, cols].bitcast(FP8X4),
-                lhsT_scale=w1_plane[a][:, cols],
-                rhs=v_codes[a, c].bitcast(FP8X4),
-                rhs_scale=v_plane[4 * a : P, c * S_HALF : (c + 1) * S_HALF],
-                start=(a == 0),
-                stop=(a == 1),
-            )
-
-        for t in range(PACK):
-            for c in range(HALVES):
-                pre[t, c] = psum.tile([P, S_HALF], F32, name="pre%d_%d" % (t, c), tag="bank%d_%d" % (t, c))
-                first_product(0, t, c)
-
-        v_codes1 = tile([P, S], U32, "v_codes1", tag="tab_plane")
-        for c in range(HALVES):
-            v_codes[1, c] = v_codes1[:, c * S_HALF : (c + 1) * S_HALF]
-            nc.vector.tensor_copy(v_codes[1, c], tab_sb[1][:].indirect(offs_half(c)))
-        deal_weight(nc.scalar.copy, w1_raw1[0], w1_bf[1], 0, H // 2)
-        deal_weight(nc.vector.tensor_copy, w1_raw1[1], w1_bf[1], H // 2, H // 2)
-        for t0, t1 in ((0, 1), (1, PACK)):
-            cols = slice(t0 * P, t1 * P)
-            nc.vector.quantize_mx(
-                w1_codes[1][:, cols].bitcast(FP8X4),
-                w1_plane[1][:, cols],
-                w1_bf[1][:, t0:t1, :].rearrange("p t x -> p (t x)"),
-            )
-            for t in range(t0, t1):
-                for c in range(HALVES):
-                    first_product(1, t, c)
-
-        w4_plane = tile([P, H], U8, "w4_plane")
-        nc.gpsimd.tensor_copy(
-            w4_plane[:].rearrange("p (t m) -> p t m", t=PACK),
+        nc.vector.tensor_copy(
+            w4_plane.rearrange("p (t m) -> p t m", t=PACK),
             w4_plane_raw[:].rearrange("p (m t) -> p t m", t=PACK),
         )
 
-        w2_bf = tile([P, PACK, H], BF16, "w2_bf")
-        deal_weight(nc.vector.tensor_copy, w2_raw[0], w2_bf, 0, H // 2)
+        pre = {}
+        for a in range(2):
+            for c in range(HALVES):
+                v_codes = tile([P, S_HALF], U32, "v_codes%d_%d" % (a, c))
+                nc.vector.tensor_copy(v_codes[:], tab_sb[a][:].indirect(offs_half(c)))
+                for t in range(PACK):
+                    if a == 0:
+                        pre[t, c] = psum.tile([P, S_HALF], F32, name="pre%d_%d" % (t, c), tag="bank%d_%d" % (t, c))
+                    cols = slice(t * P, (t + 1) * P)
+                    nc.tensor.matmul_mx(
+                        pre[t, c][:],
+                        lhsT=w1_codes[a][:, cols].bitcast(FP8X4),
+                        lhsT_scale=w1_plane[a][:, cols],
+                        rhs=v_codes[:].bitcast(FP8X4),
+                        rhs_scale=v_plane[4 * a : P, c * S_HALF : (c + 1) * S_HALF],
+                        start=(a == 0),
+                        stop=(a == 1),
+                    )
 
         h = [tile([P, S], F32, "h%d" % t) for t in range(PACK)]
         x32 = tile([P, PACK, M], F32, "x32")
-        for t in range(PACK):
-            gain_t = gain_sb[:, t : t + 1]
-            for c in range(HALVES):
-                cols = slice(c * S_HALF, (c + 1) * S_HALF)
-                nc.scalar.activation(h[t][:, cols], pre[t, c][:], ACT.Tanh, bias=b1_sb[:, t : t + 1])
-                if t == 0:
-                    nc.vector.tensor_scalar(h[t][:, cols], h[t][:, cols], gain_t, None, MULT)
-            if t == PACK - 1:
-                for c in range(HALVES):
-                    cols = slice(c * S_HALF, (c + 1) * S_HALF)
-                    nc.scalar.activation(h[t][:, cols], h[t][:, cols], ACT.Copy, scale=gain_t)
-            elif t > 0:
-                nc.vector.tensor_scalar(h[t][:], h[t][:], gain_t, None, MULT)
+        w2_bf = tile([P, PACK, H], BF16, "w2_bf", tag="tab_sb1")
+
+        def tanh_half(t, c):
+            cols = slice(c * S_HALF, (c + 1) * S_HALF)
+            nc.scalar.activation(h[t][:, cols], pre[t, c][:], ACT.Tanh, bias=b1_sb[:, t : t + 1])
+
+        def gain_on_vector(t, cols):
+            nc.vector.tensor_scalar(h[t][:, cols], h[t][:, cols], gain_sb[:, t : t + 1], None, MULT)
+
+        def pick_x(t):
             nc.vector.tensor_copy(x32[:, t, :], h[t][:].indirect(pos_sb[:]))
+
+        tanh_half(0, 0)
+        tanh_half(1, 0)
+        gain_on_vector(0, slice(0, S_HALF))
+        deal_weight(nc.vector.tensor_copy, w2_raw[0], w2_bf, 0, H // 2, "p m u j e")
+        tanh_half(0, 1)
+        gain_on_vector(0, slice(S_HALF, S))
+        pick_x(0)
+        tanh_half(1, 1)
+        gain_on_vector(1, slice(0, S))
+        pick_x(1)
+        for t in (2, 3):
+            for c in range(HALVES):
+                tanh_half(t, c)
+        for t in (2, 3):
+            nc.scalar.activation(h[t][:], h[t][:], ACT.Copy, scale=gain_sb[:, t : t + 1])
+            pick_x(t)
 
         w2_codes = tile([P, H], U32, "w2_codes")
         w2_plane = tile([P, H], U8, "w2_plane")
-        deal_weight(nc.scalar.copy, w2_raw[1], w2_bf, H // 2, H // 2)
-        nc.vector.quantize_mx(w2_codes[:].bitcast(FP8X4), w2_plane[:], w2_bf[:].rearrange("p t x -> p (t x)"))
+        deal_weight(nc.scalar.copy, w2_raw[1], w2_bf, H // 2, H // 2, "p u m j e")
+
+        def fill_page(t, tag):
+            page = tile([P, S], F32, "page%d" % t, tag=tag)
+            nc.scalar.activation(page[:], h[t][:], ACT.Copy, scale=skip_sb[:, t : t + 1])
+            return page
 
         z = {}
         for c in range(HALVES):
             cols = slice(c * M_HALF, (c + 1) * M_HALF)
-            both_bf = tile([P, 2, PACK * M_HALF], BF16, "both_bf%d" % c)
-            x_planes = x32[:, :, cols].rearrange("p t (g i) -> p g t i", i=4)
-            nc.scalar.copy(both_bf[:, 0, :].rearrange("p (g i t) -> p g t i", i=4, t=PACK), x_planes)
+            x_bf = tile([P, PACK * M_HALF], BF16, "x_bf%d" % c)
+            tint_bf = tile([P, PACK * M_HALF], BF16, "tint_bf%d" % c, tag="tint_bf")
+            nc.scalar.copy(
+                x_bf[:].rearrange("p (g i t) -> p g t i", i=4, t=PACK),
+                x32[:, :, cols].rearrange("p t (g i) -> p g t i", i=4),
+            )
             nc.vector.tensor_tensor(
-                both_bf[:, 1, :].rearrange("p (g i t) -> p g t i", i=4, t=PACK),
-                x_planes,
-                pig_sb[:, :, cols].rearrange("p t (g i) -> p g t i", i=4),
+                tint_bf[:].rearrange("p (g i t) -> p g t i", i=2, t=PACK),
+                x32[:, :, cols].rearrange("p t (g i) -> p g t i", i=2),
+                pig_sb[:, :, cols].rearrange("p t (g i) -> p g t i", i=2),
                 MULT,
             )
-            both_codes = tile([P, 2, M_HALF], U32, "both_codes%d" % c)
-            both_plane = tile([P, 2, M_HALF], U8, "both_plane%d" % c)
-            nc.vector.quantize_mx(
-                both_codes[:].rearrange("p s m -> p (s m)").bitcast(FP8X4),
-                both_plane[:].rearrange("p s m -> p (s m)"),
-                both_bf[:].rearrange("p s x -> p (s x)"),
-            )
+            if c == 0:
+                nc.vector.quantize_mx(w2_codes[:].bitcast(FP8X4), w2_plane[:], w2_bf[:].rearrange("p t x -> p (t x)"))
+            x_codes = tile([P, M_HALF], U32, "x_codes%d" % c)
+            x_plane = tile([P, M_HALF], U8, "x_plane%d" % c)
+            tint_codes = tile([P, M_HALF], U32, "tint_codes%d" % c)
+            tint_plane = tile([P, M_HALF], U8, "tint_plane%d" % c)
+            nc.vector.quantize_mx(x_codes[:].bitcast(FP8X4), x_plane[:], x_bf[:])
+            nc.vector.quantize_mx(tint_codes[:].bitcast(FP8X4), tint_plane[:], tint_bf[:])
             for t in range(PACK):
                 z[t, c] = psum.tile([P, M_HALF], F32, name="z%d_%d" % (t, c), tag="bank%d_%d" % (t, c))
                 nc.tensor.matmul_mx(
                     z[t, c][:],
                     lhsT=w4_codes[:, 2 * P * t : 2 * P * (t + 1)].bitcast(FP4X4),
                     lhsT_scale=w4_plane[:, P * t : P * (t + 1)],
-                    rhs=both_codes[:, 0, :].bitcast(FP8X4),
-                    rhs_scale=both_plane[:, 0, :],
+                    rhs=x_codes[:].bitcast(FP8X4),
+                    rhs_scale=x_plane[:],
                     start=True,
                     stop=False,
                 )
@@ -227,28 +211,42 @@ def tile_list_fresco_loss_inpainting_kernel(
                     z[t, c][:],
                     lhsT=w2_codes[:, P * t : P * (t + 1)].bitcast(FP8X4),
                     lhsT_scale=w2_plane[:, P * t : P * (t + 1)],
-                    rhs=both_codes[:, 1, :].bitcast(FP8X4),
-                    rhs_scale=both_plane[:, 1, :],
+                    rhs=tint_codes[:].bitcast(FP8X4),
+                    rhs_scale=tint_plane[:],
                     start=False,
                     stop=True,
                 )
 
         out_rows = out.rearrange("(p t) j -> p t j", t=PACK)
-        for t in range(PACK):
-            page = tile([P, S], F32, "page%d" % t, tag="w2_bf" if t == 0 else "half_tanh%d" % (t - 1))
-            nc.scalar.activation(page[:], h[t][:], ACT.Copy, scale=skip_sb[:, t : t + 1])
-            half_tanh = tile([P, M], F32, "half_tanh%d" % t)
-            y = tile([P, M], F32, "y%d" % t)
-            pieces = [(c, c + 1) for c in range(HALVES)] if t == 0 else [(0, HALVES)]
-            for c0, c1 in pieces:
-                for c in range(c0, c1):
-                    nc.scalar.activation(half_tanh[:, c * M_HALF : (c + 1) * M_HALF], z[t, c][:], ACT.Tanh, scale=0.5)
-                cols = slice(c0 * M_HALF, c1 * M_HALF)
-                nc.scalar.activation(y[:, cols], half_tanh[:, cols], ACT.Copy, bias=0.5, scale=0.5)
-                nc.vector.tensor_tensor(
-                    page[:].indirect(pos_sb[:, c0 * M_HALF // LIST_ROWS : c1 * M_HALF // LIST_ROWS]),
-                    y[:, cols],
-                    wgo_sb[:, t * M + c0 * M_HALF : t * M + c1 * M_HALF],
-                    MULT,
-                )
+        half_tanh = [tile([P, M], F32, "half_tanh%d" % t) for t in range(PACK)]
+        y = [tile([P, M], F32, "y%d" % t) for t in range(PACK)]
+
+        def tanh_of_half_z(t, c):
+            nc.scalar.activation(half_tanh[t][:, c * M_HALF : (c + 1) * M_HALF], z[t, c][:], ACT.Tanh, scale=0.5)
+
+        def put(page, t, m0, m1):
+            nc.scalar.activation(y[t][:, m0:m1], half_tanh[t][:, m0:m1], ACT.Copy, bias=0.5, scale=0.5)
+            nc.vector.tensor_tensor(
+                page[:].indirect(pos_sb[:, m0 // LIST_ROWS : m1 // LIST_ROWS]),
+                y[t][:, m0:m1],
+                wgo_sb[:, t * M + m0 : t * M + m1],
+                MULT,
+            )
+
+        page0 = fill_page(0, "w2_raw1")
+        tanh_of_half_z(0, 0)
+        tanh_of_half_z(1, 0)
+        put(page0, 0, 0, M_HALF)
+        page1 = fill_page(1, "x_bf1")
+        tanh_of_half_z(0, 1)
+        tanh_of_half_z(1, 1)
+        put(page0, 0, M_HALF, M)
+        nc.sync.dma_start(out_rows[:, 0, :], page0[:])
+        put(page1, 1, 0, M)
+        nc.sync.dma_start(out_rows[:, 1, :], page1[:])
+        for t in (2, 3):
+            page = fill_page(t, "half_tanh%d" % (t - 1))
+            for c in range(HALVES):
+                tanh_of_half_z(t, c)
+            put(page, t, 0, M)
             nc.sync.dma_start(out_rows[:, t, :], page[:])

@@ -18,6 +18,9 @@ ACT = mybir.ActivationFunctionType
 
 P = 128
 PACK = 4
+PASSES = K // (P * PACK)
+BLOCKS = 16
+QUADRANT = 32
 HALVES = 2
 S_HALF = S // HALVES
 M_HALF = M // HALVES
@@ -46,61 +49,86 @@ def tile_list_fresco_loss_inpainting_kernel(
         offs_sb = lists.tile([P, S // LIST_ROWS], U16, name="offs_sb")
         pos_sb = lists.tile([P, M // LIST_ROWS], U16, name="pos_sb")
 
-        tab_plane = tile([P, T], U8, "tab_plane")
+        tab_rows = tile([P, T], U8, "tab_rows")
         w4_plane_raw = tile([P, H], U8, "w4_plane_raw")
-        nc.vector.memset(tab_plane[:].bitcast(I32), 0)
+        for first, last in ((QUADRANT, 2 * QUADRANT), (2 * QUADRANT, P)):
+            nc.vector.memset(tab_rows[first:last, :].bitcast(I32), 0)
         nc.gpsimd.memset(w4_plane_raw[:].bitcast(I32), 0)
 
-        tab_sb = [tile([P, T], U32, "tab_sb%d" % a) for a in range(2)]
-        w1_raw = [tile([P, PACK, H], F32, "w1_raw%d" % a) for a in range(2)]
+        tab_sb0 = tile([P, T], U32, "tab_sb0")
+        w1_raw = [tile([P, PACK, H], F32, "w1_raw%d" % a) for a in range(PASSES)]
         w1_rows = w1.rearrange("(a p j) r -> a p j r", p=P, j=PACK)
         b1_sb = tile([P, PACK], F32, "b1_sb")
         gain_sb = tile([P, PACK], F32, "gain_sb")
         skip_sb = tile([P, PACK], F32, "skip_sb")
         w4_raw = tile([P, 2 * H], U8, "w4_raw")
-        pig_sb = tile([P, PACK, M], F32, "pig_sb")
-        w2_raw = [tile([P, PACK, H // 2], F32, "w2_raw%d" % c) for c in range(2)]
-        w2_rows = w2.rearrange("(p j) n -> p j n", j=PACK)
-        wgo_sb = tile([P, PACK * M], F32, "wgo_sb")
 
         def tab_pass(a):
             return tab_words[a].rearrange("p n i -> p (n i)").bitcast(I32)
 
-        for a in range(2):
-            nc.sync.dma_start(w1_raw[a][:], w1_rows[a])
+        nc.sync.dma_start(
+            tab_rows[: PASSES * BLOCKS, :].bitcast(I32), tab_scales.rearrange("a q n -> (a q) n").bitcast(I32)
+        )
         nc.sync.dma_start(offs_sb[:], offs)
-        for a in range(2):
-            nc.sync.dma_start(tab_sb[a][:].bitcast(I32), tab_pass(a))
-        for q in range(4):
-            nc.gpsimd.dma_start(
-                tab_plane[32 * q : 32 * q + 8, :].bitcast(I32), tab_scales[:, 4 * q : 4 * q + 4, :].bitcast(I32)
-            )
-        nc.gpsimd.dma_start(w4_raw[:].bitcast(I32), w4_words[0].bitcast(I32))
+        nc.sync.dma_start(tab_sb0[:].bitcast(I32), tab_pass(0))
+        nc.sync.dma_start(w4_raw[:].bitcast(I32), w4_words[0].bitcast(I32))
         for r in range(4):
-            nc.gpsimd.dma_start(w4_plane_raw[r:P:32, :].bitcast(I32), w4_scales[0, r:16:4, :].bitcast(I32))
-        for vec_sb, vec in ((b1_sb, b1), (gain_sb, gain), (skip_sb, skip)):
-            nc.sync.dma_start(vec_sb[:], vec.rearrange("(p t) -> p t", t=PACK))
+            nc.sync.dma_start(w4_plane_raw[r:P:QUADRANT, :].bitcast(I32), w4_scales[0, r:BLOCKS:4, :].bitcast(I32))
+        for a in range(PASSES):
+            nc.sync.dma_start(w1_raw[a][:], w1_rows[a])
         nc.sync.dma_start(pos_sb[:], pos1)
-        nc.sync.dma_start(w2_raw[0][:], w2_rows[:, :, : H // 2])
-        nc.sync.dma_start(pig_sb[:], pigment.rearrange("(p t) m -> p t m", t=PACK))
-        nc.sync.dma_start(w2_raw[1][:], w2_rows[:, :, H // 2 :])
-        wgo_rows = wgo.rearrange("(q t) m -> q (t m)", t=PACK)
-        for q in range(4):
-            nc.sync.dma_start(wgo_sb[32 * q : 32 * (q + 1), :], wgo_rows)
+        for vec_sb, vec in ((b1_sb, b1), (gain_sb, gain), (skip_sb, skip)):
+            nc.gpsimd.dma_start(vec_sb[:], vec.rearrange("(p t) -> p t", t=PACK))
 
         def offs_half(c):
             n = S_HALF // LIST_ROWS
             return offs_sb[:, c * n : (c + 1) * n]
 
-        v_plane = tile([P, S], U8, "v_plane")
-        nc.vector.tensor_copy(v_plane[:], tab_plane[:].indirect(offs_sb[:]))
+        v_rows = tile([P, S], U8, "v_rows")
+        nc.vector.tensor_copy(v_rows[:], tab_rows[:].indirect(offs_sb[:]))
+        v_plane = [tile([P, S], U8, "v_plane%d" % a) for a in range(PASSES)]
 
-        w1_codes = [tile([P, H], U32, "w1_codes%d" % a) for a in range(2)]
-        w1_plane = [tile([P, H], U8, "w1_plane%d" % a) for a in range(2)]
-        for a in range(2):
+        def carry_scale_rows(a):
+            for r in range(4):
+                nc.sync.dma_start(
+                    v_plane[a][r:P:QUADRANT, :].bitcast(I32),
+                    v_rows[BLOCKS * a + r : BLOCKS * (a + 1) : 4, :].bitcast(I32),
+                )
+
+        carry_scale_rows(0)
+        tab_sb1 = tile([P, T], U32, "tab_sb1", tag="tab_rows")
+        nc.sync.dma_start(tab_sb1[:].bitcast(I32), tab_pass(1))
+        carry_scale_rows(1)
+        tab_sb = (tab_sb0, tab_sb1)
+
+        w1_codes = [tile([P, H], U32, "w1_codes%d" % a) for a in range(PASSES)]
+        w1_plane = [tile([P, H], U8, "w1_plane%d" % a) for a in range(PASSES)]
+        for a in range(PASSES):
             w1_bf = tile([P, PACK, H], BF16, "w1_bf%d" % a)
             deal_weight(nc.scalar.copy, w1_raw[a], w1_bf, 0, H, "p u m j e")
             nc.vector.quantize_mx(w1_codes[a][:].bitcast(FP8X4), w1_plane[a][:], w1_bf[:].rearrange("p t x -> p (t x)"))
+
+        pre = {}
+
+        def first_stage_pass(a):
+            for c in range(HALVES):
+                v_codes = tile([P, S_HALF], U32, "v_codes%d_%d" % (a, c))
+                nc.vector.tensor_copy(v_codes[:], tab_sb[a][:].indirect(offs_half(c)))
+                for t in range(PACK):
+                    if a == 0:
+                        pre[t, c] = psum.tile([P, S_HALF], F32, name="pre%d_%d" % (t, c), tag="bank%d_%d" % (t, c))
+                    cols = slice(t * P, (t + 1) * P)
+                    nc.tensor.matmul_mx(
+                        pre[t, c][:],
+                        lhsT=w1_codes[a][:, cols].bitcast(FP8X4),
+                        lhsT_scale=w1_plane[a][:, cols],
+                        rhs=v_codes[:].bitcast(FP8X4),
+                        rhs_scale=v_plane[a][:, c * S_HALF : (c + 1) * S_HALF],
+                        start=(a == 0),
+                        stop=(a == PASSES - 1),
+                    )
+
+        first_stage_pass(0)
 
         w4_dealt = tile([P, 3 * H], U8, "w4_dealt", tag="tab_sb0")
         w4_codes = w4_dealt[:, : 2 * H]
@@ -114,45 +142,42 @@ def tile_list_fresco_loss_inpainting_kernel(
             w4_plane_raw[:].rearrange("p (m t) -> p t m", t=PACK),
         )
 
-        pre = {}
-        for a in range(2):
-            for c in range(HALVES):
-                v_codes = tile([P, S_HALF], U32, "v_codes%d_%d" % (a, c))
-                nc.vector.tensor_copy(v_codes[:], tab_sb[a][:].indirect(offs_half(c)))
-                for t in range(PACK):
-                    if a == 0:
-                        pre[t, c] = psum.tile([P, S_HALF], F32, name="pre%d_%d" % (t, c), tag="bank%d_%d" % (t, c))
-                    cols = slice(t * P, (t + 1) * P)
-                    nc.tensor.matmul_mx(
-                        pre[t, c][:],
-                        lhsT=w1_codes[a][:, cols].bitcast(FP8X4),
-                        lhsT_scale=w1_plane[a][:, cols],
-                        rhs=v_codes[:].bitcast(FP8X4),
-                        rhs_scale=v_plane[4 * a : P, c * S_HALF : (c + 1) * S_HALF],
-                        start=(a == 0),
-                        stop=(a == 1),
-                    )
+        first_stage_pass(1)
+
+        w2_rows = w2.rearrange("(p j) n -> p j n", j=PACK)
+        w2_raw = [tile([P, PACK, H // 2], F32, "w2_raw%d" % c, tag=("w1_raw0", "w1_bf1")[c]) for c in range(2)]
+        pig_sb = tile([P, PACK, M], F32, "pig_sb", tag="w1_raw1")
+        wgo_sb = tile([P, PACK * M], F32, "wgo_sb", tag="v_codes0_1")
+        nc.sync.dma_start(w2_raw[0][:], w2_rows[:, :, : H // 2])
+        nc.sync.dma_start(pig_sb[:], pigment.rearrange("(p t) m -> p t m", t=PACK))
+        nc.sync.dma_start(w2_raw[1][:], w2_rows[:, :, H // 2 :])
+        wgo_rows = wgo.rearrange("(q t) m -> q (t m)", t=PACK)
+        for q in range(P // QUADRANT):
+            nc.sync.dma_start(wgo_sb[QUADRANT * q : QUADRANT * (q + 1), :], wgo_rows)
 
         h = [tile([P, S], F32, "h%d" % t) for t in range(PACK)]
         x32 = tile([P, PACK, M], F32, "x32")
-        w2_bf = tile([P, PACK, H], BF16, "w2_bf", tag="tab_sb1")
+        w2_bf = tile([P, PACK, H], BF16, "w2_bf", tag="tab_rows")
+        low, high = slice(0, S_HALF), slice(S_HALF, S)
 
         def tanh_half(t, c):
-            cols = slice(c * S_HALF, (c + 1) * S_HALF)
-            nc.scalar.activation(h[t][:, cols], pre[t, c][:], ACT.Tanh, bias=b1_sb[:, t : t + 1])
+            nc.scalar.activation(h[t][:, (low, high)[c]], pre[t, c][:], ACT.Tanh, bias=b1_sb[:, t : t + 1])
 
         def gain_on_vector(t, cols):
             nc.vector.tensor_scalar(h[t][:, cols], h[t][:, cols], gain_sb[:, t : t + 1], None, MULT)
+
+        def gain_on_scalar(t, cols):
+            nc.scalar.activation(h[t][:, cols], h[t][:, cols], ACT.Copy, scale=gain_sb[:, t : t + 1])
 
         def pick_x(t):
             nc.vector.tensor_copy(x32[:, t, :], h[t][:].indirect(pos_sb[:]))
 
         tanh_half(0, 0)
         tanh_half(1, 0)
-        gain_on_vector(0, slice(0, S_HALF))
+        gain_on_vector(0, low)
         deal_weight(nc.vector.tensor_copy, w2_raw[0], w2_bf, 0, H // 2, "p m u j e")
         tanh_half(0, 1)
-        gain_on_vector(0, slice(S_HALF, S))
+        gain_on_vector(0, high)
         pick_x(0)
         tanh_half(1, 1)
         gain_on_vector(1, slice(0, S))
@@ -161,7 +186,7 @@ def tile_list_fresco_loss_inpainting_kernel(
             for c in range(HALVES):
                 tanh_half(t, c)
         for t in (2, 3):
-            nc.scalar.activation(h[t][:], h[t][:], ACT.Copy, scale=gain_sb[:, t : t + 1])
+            gain_on_scalar(t, slice(0, S))
             pick_x(t)
 
         w2_codes = tile([P, H], U32, "w2_codes")
@@ -233,7 +258,7 @@ def tile_list_fresco_loss_inpainting_kernel(
                 MULT,
             )
 
-        page0 = fill_page(0, "w2_raw1")
+        page0 = fill_page(0, "w1_bf1")
         tanh_of_half_z(0, 0)
         tanh_of_half_z(1, 0)
         put(page0, 0, 0, M_HALF)

from contextlib import ExitStack

import concourse.mybir as mybir

K, H, T, S, M = 1024, 512, 4096, 1024, 512
FLOPS = 2 * K * H * S + 2 * 2 * H * H * M

F32 = mybir.dt.float32
BF16 = mybir.dt.bfloat16
I32 = mybir.dt.int32
U32 = mybir.dt.uint32
U16 = mybir.dt.uint16
U8 = mybir.dt.uint8
FP8X4 = mybir.dt.float8_e4m3fn_x4
FP4X4 = mybir.dt.float4_e2m1fn_x4
MULT = mybir.AluOpType.mult
ACT = mybir.ActivationFunctionType

P = 128
PACK = 4
PASSES = K // (P * PACK)
BLOCKS = 16
QUADRANT = 32
HALVES = 2
S_HALF = S // HALVES
M_HALF = M // HALVES
LIST_ROWS = 16


def deal_weight(engine_copy, raw, grouped, col0, cols, order):
    engine_copy(
        grouped[:, :, col0 : col0 + cols].rearrange("p (u e) (m j) -> " + order, e=2, j=PACK),
        raw[:].rearrange("p j (m u e) -> " + order, u=2, e=2),
    )


def tile_list_fresco_loss_inpainting_kernel(
    tc, tab_words, tab_scales, offs, pos1, w1, b1, gain, pigment, w4_words, w4_scales, w2, skip, wgo, out
):
    nc = tc.nc
    with ExitStack() as ctx:
        lists = ctx.enter_context(tc.tile_pool(name="lists", bufs=1))
        sb = ctx.enter_context(tc.tile_pool(name="sb", bufs=1))
        psum = ctx.enter_context(tc.psum_pool(name="psum", bufs=1))

        def tile(shape, dtype, name, tag=None):
            return sb.tile(shape, dtype, name=name, tag=tag or name, align_bytes=64)

        offs_sb = lists.tile([P, S // LIST_ROWS], U16, name="offs_sb")
        pos_sb = lists.tile([P, M // LIST_ROWS], U16, name="pos_sb")

        tab_rows = tile([P, T], U8, "tab_rows")
        w4_plane_raw = tile([P, H], U8, "w4_plane_raw")
        for first, last in ((QUADRANT, 2 * QUADRANT), (2 * QUADRANT, P)):
            nc.vector.memset(tab_rows[first:last, :].bitcast(I32), 0)
        nc.gpsimd.memset(w4_plane_raw[:].bitcast(I32), 0)

        tab_sb0 = tile([P, T], U32, "tab_sb0")
        w1_raw = [tile([P, PACK, H], F32, "w1_raw%d" % a) for a in range(PASSES)]
        w1_rows = w1.rearrange("(a p j) r -> a p j r", p=P, j=PACK)
        b1_sb = tile([P, PACK], F32, "b1_sb")
        gain_sb = tile([P, PACK], F32, "gain_sb")
        skip_sb = tile([P, PACK], F32, "skip_sb")
        w4_raw = tile([P, 2 * H], U8, "w4_raw")

        def tab_pass(a):
            return tab_words[a].rearrange("p n i -> p (n i)").bitcast(I32)

        nc.sync.dma_start(
            tab_rows[: PASSES * BLOCKS, :].bitcast(I32), tab_scales.rearrange("a q n -> (a q) n").bitcast(I32)
        )
        nc.sync.dma_start(offs_sb[:], offs)
        nc.sync.dma_start(tab_sb0[:].bitcast(I32), tab_pass(0))
        nc.sync.dma_start(w4_raw[:].bitcast(I32), w4_words[0].bitcast(I32))
        for r in range(4):
            nc.sync.dma_start(w4_plane_raw[r:P:QUADRANT, :].bitcast(I32), w4_scales[0, r:BLOCKS:4, :].bitcast(I32))
        for a in range(PASSES):
            nc.sync.dma_start(w1_raw[a][:], w1_rows[a])
        nc.sync.dma_start(pos_sb[:], pos1)
        for vec_sb, vec in ((b1_sb, b1), (gain_sb, gain), (skip_sb, skip)):
            nc.gpsimd.dma_start(vec_sb[:], vec.rearrange("(p t) -> p t", t=PACK))

        def offs_half(c):
            n = S_HALF // LIST_ROWS
            return offs_sb[:, c * n : (c + 1) * n]

        v_rows = tile([P, S], U8, "v_rows")
        nc.vector.tensor_copy(v_rows[:], tab_rows[:].indirect(offs_sb[:]))
        v_plane = [tile([P, S], U8, "v_plane%d" % a) for a in range(PASSES)]

        def carry_scale_rows(a):
            for r in range(4):
                nc.sync.dma_start(
                    v_plane[a][r:P:QUADRANT, :].bitcast(I32),
                    v_rows[BLOCKS * a + r : BLOCKS * (a + 1) : 4, :].bitcast(I32),
                )

        carry_scale_rows(0)
        tab_sb1 = tile([P, T], U32, "tab_sb1", tag="tab_rows")
        nc.sync.dma_start(tab_sb1[:].bitcast(I32), tab_pass(1))
        carry_scale_rows(1)
        tab_sb = (tab_sb0, tab_sb1)

        w1_codes = [tile([P, H], U32, "w1_codes%d" % a) for a in range(PASSES)]
        w1_plane = [tile([P, H], U8, "w1_plane%d" % a) for a in range(PASSES)]
        for a in range(PASSES):
            w1_bf = tile([P, PACK, H], BF16, "w1_bf%d" % a)
            deal_weight(nc.scalar.copy, w1_raw[a], w1_bf, 0, H, "p u m j e")
            nc.vector.quantize_mx(w1_codes[a][:].bitcast(FP8X4), w1_plane[a][:], w1_bf[:].rearrange("p t x -> p (t x)"))

        pre = {}

        def first_stage_pass(a):
            for c in range(HALVES):
                v_codes = tile([P, S_HALF], U32, "v_codes%d_%d" % (a, c))
                nc.vector.tensor_copy(v_codes[:], tab_sb[a][:].indirect(offs_half(c)))
                for t in range(PACK):
                    if a == 0:
                        pre[t, c] = psum.tile([P, S_HALF], F32, name="pre%d_%d" % (t, c), tag="bank%d_%d" % (t, c))
                    cols = slice(t * P, (t + 1) * P)
                    nc.tensor.matmul_mx(
                        pre[t, c][:],
                        lhsT=w1_codes[a][:, cols].bitcast(FP8X4),
                        lhsT_scale=w1_plane[a][:, cols],
                        rhs=v_codes[:].bitcast(FP8X4),
                        rhs_scale=v_plane[a][:, c * S_HALF : (c + 1) * S_HALF],
                        start=(a == 0),
                        stop=(a == PASSES - 1),
                    )

        first_stage_pass(0)

        w4_dealt = tile([P, 3 * H], U8, "w4_dealt", tag="tab_sb0")
        w4_codes = w4_dealt[:, : 2 * H]
        w4_plane = w4_dealt[:, 2 * H :]
        nc.vector.tensor_copy(
            w4_codes.bitcast(U16).rearrange("p (t m) -> p t m", t=PACK),
            w4_raw[:].bitcast(U16).rearrange("p (m t) -> p t m", t=PACK),
        )
        nc.vector.tensor_copy(
            w4_plane.rearrange("p (t m) -> p t m", t=PACK),
            w4_plane_raw[:].rearrange("p (m t) -> p t m", t=PACK),
        )

        first_stage_pass(1)

        w2_rows = w2.rearrange("(p j) n -> p j n", j=PACK)
        w2_raw = [tile([P, PACK, H // 2], F32, "w2_raw%d" % c, tag=("w1_raw0", "w1_bf1")[c]) for c in range(2)]
        pig_sb = tile([P, PACK, M], F32, "pig_sb", tag="w1_raw1")
        wgo_sb = tile([P, PACK * M], F32, "wgo_sb", tag="v_codes0_1")
        nc.sync.dma_start(w2_raw[0][:], w2_rows[:, :, : H // 2])
        nc.sync.dma_start(pig_sb[:], pigment.rearrange("(p t) m -> p t m", t=PACK))
        nc.sync.dma_start(w2_raw[1][:], w2_rows[:, :, H // 2 :])
        wgo_rows = wgo.rearrange("(q t) m -> q (t m)", t=PACK)
        for q in range(P // QUADRANT):
            nc.sync.dma_start(wgo_sb[QUADRANT * q : QUADRANT * (q + 1), :], wgo_rows)

        h = [tile([P, S], F32, "h%d" % t) for t in range(PACK)]
        x32 = tile([P, PACK, M], F32, "x32")
        w2_bf = tile([P, PACK, H], BF16, "w2_bf", tag="tab_rows")
        low, high = slice(0, S_HALF), slice(S_HALF, S)

        def tanh_half(t, c):
            nc.scalar.activation(h[t][:, (low, high)[c]], pre[t, c][:], ACT.Tanh, bias=b1_sb[:, t : t + 1])

        def gain_on_vector(t, cols):
            nc.vector.tensor_scalar(h[t][:, cols], h[t][:, cols], gain_sb[:, t : t + 1], None, MULT)

        def gain_on_scalar(t, cols):
            nc.scalar.activation(h[t][:, cols], h[t][:, cols], ACT.Copy, scale=gain_sb[:, t : t + 1])

        def pick_x(t):
            nc.vector.tensor_copy(x32[:, t, :], h[t][:].indirect(pos_sb[:]))

        tanh_half(0, 0)
        tanh_half(1, 0)
        gain_on_vector(0, low)
        deal_weight(nc.vector.tensor_copy, w2_raw[0], w2_bf, 0, H // 2, "p m u j e")
        tanh_half(0, 1)
        gain_on_vector(0, high)
        pick_x(0)
        tanh_half(1, 1)
        gain_on_vector(1, slice(0, S))
        pick_x(1)
        for t in (2, 3):
            for c in range(HALVES):
                tanh_half(t, c)
        for t in (2, 3):
            gain_on_scalar(t, slice(0, S))
            pick_x(t)

        w2_codes = tile([P, H], U32, "w2_codes")
        w2_plane = tile([P, H], U8, "w2_plane")
        deal_weight(nc.scalar.copy, w2_raw[1], w2_bf, H // 2, H // 2, "p u m j e")

        def fill_page(t, tag):
            page = tile([P, S], F32, "page%d" % t, tag=tag)
            nc.scalar.activation(page[:], h[t][:], ACT.Copy, scale=skip_sb[:, t : t + 1])
            return page

        z = {}
        for c in range(HALVES):
            cols = slice(c * M_HALF, (c + 1) * M_HALF)
            x_bf = tile([P, PACK * M_HALF], BF16, "x_bf%d" % c)
            tint_bf = tile([P, PACK * M_HALF], BF16, "tint_bf%d" % c, tag="tint_bf")
            nc.scalar.copy(
                x_bf[:].rearrange("p (g i t) -> p g t i", i=4, t=PACK),
                x32[:, :, cols].rearrange("p t (g i) -> p g t i", i=4),
            )
            nc.vector.tensor_tensor(
                tint_bf[:].rearrange("p (g i t) -> p g t i", i=2, t=PACK),
                x32[:, :, cols].rearrange("p t (g i) -> p g t i", i=2),
                pig_sb[:, :, cols].rearrange("p t (g i) -> p g t i", i=2),
                MULT,
            )
            if c == 0:
                nc.vector.quantize_mx(w2_codes[:].bitcast(FP8X4), w2_plane[:], w2_bf[:].rearrange("p t x -> p (t x)"))
            x_codes = tile([P, M_HALF], U32, "x_codes%d" % c)
            x_plane = tile([P, M_HALF], U8, "x_plane%d" % c)
            tint_codes = tile([P, M_HALF], U32, "tint_codes%d" % c)
            tint_plane = tile([P, M_HALF], U8, "tint_plane%d" % c)
            nc.vector.quantize_mx(x_codes[:].bitcast(FP8X4), x_plane[:], x_bf[:])
            nc.vector.quantize_mx(tint_codes[:].bitcast(FP8X4), tint_plane[:], tint_bf[:])
            for t in range(PACK):
                z[t, c] = psum.tile([P, M_HALF], F32, name="z%d_%d" % (t, c), tag="bank%d_%d" % (t, c))
                nc.tensor.matmul_mx(
                    z[t, c][:],
                    lhsT=w4_codes[:, 2 * P * t : 2 * P * (t + 1)].bitcast(FP4X4),
                    lhsT_scale=w4_plane[:, P * t : P * (t + 1)],
                    rhs=x_codes[:].bitcast(FP8X4),
                    rhs_scale=x_plane[:],
                    start=True,
                    stop=False,
                )
                nc.tensor.matmul_mx(
                    z[t, c][:],
                    lhsT=w2_codes[:, P * t : P * (t + 1)].bitcast(FP8X4),
                    lhsT_scale=w2_plane[:, P * t : P * (t + 1)],
                    rhs=tint_codes[:].bitcast(FP8X4),
                    rhs_scale=tint_plane[:],
                    start=False,
                    stop=True,
                )

        out_rows = out.rearrange("(p t) j -> p t j", t=PACK)
        half_tanh = [tile([P, M], F32, "half_tanh%d" % t) for t in range(PACK)]
        y = [tile([P, M], F32, "y%d" % t) for t in range(PACK)]

        def tanh_of_half_z(t, c):
            nc.scalar.activation(half_tanh[t][:, c * M_HALF : (c + 1) * M_HALF], z[t, c][:], ACT.Tanh, scale=0.5)

        def put(page, t, m0, m1):
            nc.scalar.activation(y[t][:, m0:m1], half_tanh[t][:, m0:m1], ACT.Copy, bias=0.5, scale=0.5)
            nc.vector.tensor_tensor(
                page[:].indirect(pos_sb[:, m0 // LIST_ROWS : m1 // LIST_ROWS]),
                y[t][:, m0:m1],
                wgo_sb[:, t * M + m0 : t * M + m1],
                MULT,
            )

        page0 = fill_page(0, "w1_bf1")
        tanh_of_half_z(0, 0)
        tanh_of_half_z(1, 0)
        put(page0, 0, 0, M_HALF)
        page1 = fill_page(1, "x_bf1")
        tanh_of_half_z(0, 1)
        tanh_of_half_z(1, 1)
        put(page0, 0, M_HALF, M)
        nc.sync.dma_start(out_rows[:, 0, :], page0[:])
        put(page1, 1, 0, M)
        nc.sync.dma_start(out_rows[:, 1, :], page1[:])
        for t in (2, 3):
            page = fill_page(t, "half_tanh%d" % (t - 1))
            for c in range(HALVES):
                tanh_of_half_z(t, c)
            put(page, t, 0, M)
            nc.sync.dma_start(out_rows[:, t, :], page[:])
